import numpy as np
import ml_dtypes


def mxq(x, axis, fmt="e4m3"):
    dtype, down = {"e4m3": (ml_dtypes.float8_e4m3fn, 7), "e5m2": (ml_dtypes.float8_e5m2, 14)}[fmt]
    v = np.moveaxis(np.asarray(x, np.float32).astype(ml_dtypes.bfloat16).astype(np.float64), axis, -1)
    blocks = v.reshape(v.shape[:-1] + (-1, 32))
    amax = np.abs(blocks).max(-1, keepdims=True)
    byte = np.maximum(np.where(amax > 0, np.frexp(amax)[1] - 1 + 127, 0) - down, 1)
    scale = np.exp2(byte - 127.0)
    codes = (blocks / scale).astype(np.float32).astype(dtype).astype(np.float64)
    return np.moveaxis((codes * scale).reshape(v.shape), -1, axis)


WIDE = False


def mx_kscale(k):
    if not WIDE:
        return np.ones(k)
    levels = np.array([24, -24, 12, -12, 0])
    if k % 512:
        return np.exp2(np.random.permutation(np.resize(levels, k // 32))).repeat(32)
    a = np.empty((k // 512, 16))
    for p in range(k // 512):
        a[p, :8] = np.random.permutation(np.resize(levels, 8))
        for g in range(8):
            far = levels[np.abs(levels - a[p, g]) >= 10]
            a[p, g + 8] = far[np.random.randint(len(far))]
    return np.exp2(a.ravel()).repeat(32)


def f64(x):
    return np.asarray(x).astype(np.float64)


def striped8(idx):
    return np.concatenate([v.reshape(-1, 16).T for v in idx]).astype(np.uint16)


def unstriped8(offs):
    return np.stack([offs[16 * g:16 * g + 16].T.reshape(-1) for g in range(8)]).astype(np.int64)


E2M1 = np.array([0.0, 0.5, 1.0, 1.5, 2.0, 3.0, 4.0, 6.0, -0.0, -0.5, -1.0, -1.5, -2.0, -3.0, -4.0, -6.0])


def pack_weight(w, fmt):
    k, n = w.shape
    w = f64(np.asarray(w, np.float32).astype(ml_dtypes.bfloat16)).reshape(k // 32, 32, n)
    amax = np.abs(w).max(1)
    if fmt == "e4m3":
        byte = np.frexp(amax)[1] - 1 + 127 - 7
    else:
        mant, ex = np.frexp(amax / 6.0)
        byte = np.where(mant > 0.5, ex, ex - 1) + 127
    byte = np.clip(np.where(amax > 0, byte, 1), 1, 254)
    scaled = (w * np.exp2(127.0 - byte)[:, None, :]).reshape(k, n).astype(np.float32)
    by_word = np.ascontiguousarray(scaled.reshape(k // 512, 128, 4, n).transpose(0, 1, 3, 2))
    if fmt == "e4m3":
        words = by_word.astype(ml_dtypes.float8_e4m3fn).view(np.uint8)
    else:
        c = by_word.astype(ml_dtypes.float4_e2m1fn).view(np.uint8) & 0xF
        words = (c[..., 0::2] | (c[..., 1::2] << 4)).reshape(k // 512, 128, 2 * n)
    return np.ascontiguousarray(words), np.ascontiguousarray(byte.astype(np.uint8).reshape(k // 512, 16, n))


def unpack_weight(words, scales, fmt):
    g, _, n = scales.shape
    words = np.ascontiguousarray(words).reshape(g, 128, n, -1)
    if fmt == "e4m3":
        vals = words.view(ml_dtypes.float8_e4m3fn).astype(np.float64)
    else:
        nib = np.empty((g, 128, n, 4), np.uint8)
        nib[..., 0::2] = words & 0xF
        nib[..., 1::2] = words >> 4
        vals = E2M1[nib]
    vals = vals * np.repeat(np.exp2(scales.astype(np.float64) - 127.0), 8, axis=1)[..., None]
    return vals.transpose(0, 1, 3, 2).reshape(g * 512, n)


def planes(y):
    n, m = y.shape
    v = y.astype(np.float32).astype(ml_dtypes.bfloat16).astype(np.float64).reshape(n // 32, 32, m)
    top = np.abs(v).max(1)
    byte = np.clip(np.where(top > 0, np.frexp(top)[1] - 1 + 127 - 7, 1), 1, 254)
    codes = (v * np.exp2(127.0 - byte)[:, None, :]).reshape(n, m).astype(np.float32).astype(ml_dtypes.float8_e4m3fn).view(np.uint8)
    words = codes.reshape(n // 512, 128, 4, m).transpose(0, 1, 3, 2)
    return np.ascontiguousarray(words), np.ascontiguousarray(byte.astype(np.uint8).reshape(n // 512, 16, m))


def gelu(f):
    return 0.5 * f * (1.0 + np.tanh(np.sqrt(2.0 / np.pi) * (f + 0.044715 * f**3)))


K, L, N, T, J = 1024, 512, 512, 2048, 1024


def setup_inputs():
    n = np.random.standard_normal
    s = mx_kscale(K)[:, None]
    s2 = mx_kscale(L)[:, None]
    p_wt = pack_weight(n((K, N)) / np.sqrt(K) / s, "e2m1")
    p_wx = pack_weight(n((L, N)) / np.sqrt(L) / s2, "e4m3")
    return {
        "xT": (n((K, T)) * s).astype(np.float32),
        "wgt": np.repeat(np.random.uniform(0.5, 2.0, (8, J)), 16, axis=0).astype(np.float32),
        "wt_words": p_wt[0],
        "wt_scales": p_wt[1],
        "c": (n((L, J)) * s2).astype(np.float32),
        "wx_words": p_wx[0],
        "wx_scales": p_wx[1],
        "b": (0.3 * n(N)).astype(np.float32),
        "offs": striped8(np.stack([np.random.permutation(T)[:J] for _ in range(8)])),
    }


def reference(xT, wgt, wt_words, wt_scales, c, wx_words, wx_scales, b, offs):
    idx = unstriped8(offs)
    rows = np.arange(K)
    xg = f64(wgt)[rows // 4 % 128] * f64(xT)[rows[:, None], idx[rows % 512 // 64]]
    xT_ = mxq(xg, 0, "e4m3")
    wt_ = unpack_weight(wt_words, wt_scales, "e2m1")
    c_q_ = mxq(f64(c), 0, "e4m3")
    c_r_ = mxq(f64(c) - c_q_, 0, "e4m3")
    wx_ = unpack_weight(wx_words, wx_scales, "e4m3")
    y = wt_.T @ xT_ + wx_.T @ c_q_ + wx_.T @ c_r_
    out_0 = gelu(y + f64(b)[:, None])
    return (out_0,) + planes(out_0)

@@ -1,0 +1,324 @@
+from contextlib import ExitStack
+
+import concourse.mybir as mybir
+
+K, L, N, T, J = 1024, 512, 512, 2048, 1024
+FLOPS = 2 * N * J * (K + 3 * L)
+
+F32 = mybir.dt.float32
+BF16 = mybir.dt.bfloat16
+I32 = mybir.dt.int32
+U32 = mybir.dt.uint32
+U16 = mybir.dt.uint16
+U8 = mybir.dt.uint8
+FP8X4 = mybir.dt.float8_e4m3fn_x4
+FP4X4 = mybir.dt.float4_e2m1fn_x4
+MULT = mybir.AluOpType.mult
+SUBTRACT = mybir.AluOpType.subtract
+IS_EQUAL = mybir.AluOpType.is_equal
+GELU = mybir.ActivationFunctionType.Gelu_apprx_tanh
+
+P = 128
+PACK = 4
+BANK = 512
+HALF = 512
+QUARTER = 256
+SUB = 128
+CHUNKS = [(0, 256), (256, 256), (512, 256), (768, 128), (896, 128)]
+
+
+def walk_rows(ap):
+    return ap.rearrange("p t (c i) -> p c t i", i=PACK)
+
+
+def walk_words(ap):
+    return ap.rearrange("p (c i t) -> p c t i", i=PACK, t=PACK)
+
+
+def tile_list_geluP_kernel(
+    tc, xT, wgt, wt_words, wt_scales, c, wx_words, wx_scales, b, offs, out_0, out_1, out_2
+):
+    nc = tc.nc
+
+    with ExitStack() as ctx:
+        keep = ctx.enter_context(tc.tile_pool(name="keep", bufs=1))
+        psum = ctx.enter_context(tc.psum_pool(name="psum", bufs=1))
+
+        def sb(shape, dtype, name, tag=None):
+            return keep.tile(shape, dtype, name=name, tag=tag or name, align_bytes=64)
+
+        def bank(index, shape, name):
+            return psum.tile(shape, F32, name=name, tag="bank%d" % index)
+
+        def interleave(engine, words, rows):
+            if engine == "vector":
+                nc.vector.tensor_copy(out=walk_words(words), in_=walk_rows(rows))
+            else:
+                nc.scalar.copy(out=walk_words(words), in_=walk_rows(rows))
+
+        def quantize(words, name):
+            width = words.shape[1] // PACK
+            codes = sb([P, width], U32, name + "_codes")
+            scales = sb([P, width], U8, name + "_scales")
+            nc.vector.quantize_mx(out=codes[:].bitcast(FP8X4), scales=scales[:], in_=words)
+            return codes, scales
+
+        offsets = keep.tile([P, J // 16], U16, name="offsets")
+        nc.sync.dma_start(offsets[:], offs)
+
+        distance = sb([P, P], I32, "distance")
+        nc.gpsimd.iota(distance[:], pattern=[[1, P]], base=0, channel_multiplier=-1)
+        ws_raw = sb([P, 2, N], U8, "ws_raw")
+        nc.gpsimd.memset(ws_raw[:].bitcast(I32), 0)
+
+        warm = sb([P, 8], F32, "warm")
+        nc.vector.memset(warm[:], 0.0)
+        warm2 = sb([P, 8], F32, "warm2")
+        nc.scalar.activation(out=warm2[:], in_=warm[:], func=GELU)
+
+        wx_raw = sb([P, N], U32, "wx_raw")
+        wt_raw = sb([P, 2, 2 * N], U8, "wt_raw")
+        bias = sb([P, PACK], F32, "bias")
+
+        def load_weights():
+            nc.sync.dma_start(out=wx_raw[:].bitcast(I32), in_=wx_words[0].rearrange("p n i -> p (n i)").bitcast(I32))
+            nc.sync.dma_start(out=wt_raw[:].bitcast(I32), in_=wt_words.rearrange("a p n -> p a n").bitcast(I32))
+
+        def load_scales(q):
+            nc.sync.dma_start(
+                out=ws_raw[32 * q : 32 * q + 4, :, :].bitcast(I32),
+                in_=wt_scales[:, 4 * q : 4 * q + 4, :].rearrange("a r n -> r a n").bitcast(I32),
+            )
+            nc.sync.dma_start(
+                out=ws_raw[32 * q + 4 : 32 * q + 8, 0, :].bitcast(I32),
+                in_=wx_scales[0, 4 * q : 4 * q + 4, :].bitcast(I32),
+            )
+
+        c_rows = c.rearrange("(p t) j -> p t j", t=PACK)
+        x_rows = xT.rearrange("(a p i) t -> a i p t", a=2, i=PACK)
+        c_sb = {}
+        x_sb = {}
+        wgt_sb = {}
+
+        def load_c(quarter):
+            tile = sb([P, PACK, QUARTER], F32, "c_%d" % quarter)
+            nc.sync.dma_start(out=tile[:], in_=c_rows[:, :, quarter * QUARTER : (quarter + 1) * QUARTER])
+            c_sb[quarter] = tile
+
+        def load_x(plane):
+            tile = sb([P, T], F32, "x_%d" % plane)
+            nc.sync.dma_start(out=tile[:], in_=x_rows[plane // PACK, plane % PACK])
+            x_sb[plane] = tile
+
+        def load_wgt(half):
+            tile = sb([P, HALF], F32, "wgt_%d" % half)
+            nc.sync.dma_start(out=tile[:], in_=wgt[:, half * HALF : (half + 1) * HALF])
+            wgt_sb[half] = tile
+
+        def load_bias():
+            nc.sync.dma_start(out=bias[:], in_=b.rearrange("(p t) -> p t", t=PACK))
+
+        load_weights()
+        for quarter in range(4):
+            load_c(quarter)
+        load_wgt(0)
+        load_x(0)
+        load_wgt(1)
+        for plane in range(1, 5):
+            load_scales(plane - 1)
+            load_x(plane)
+        load_bias()
+        for plane in range(5, 8):
+            load_x(plane)
+
+        id_words = sb([P, PACK, P, PACK], BF16, "id_words")
+        nc.vector.memset(id_words[:], 0.0)
+        for t in range(PACK):
+            nc.vector.tensor_single_scalar(out=id_words[:, t, :, t], in_=distance[:], scalar=0.0, op=IS_EQUAL)
+        id_codes, id_scales = quantize(id_words[:].rearrange("p t m i -> p (t m i)"), "id")
+
+        wx_dealt = sb([P, PACK, P], U32, "wx_dealt")
+        wt_dealt = sb([P, 2, PACK, 2 * P], U8, "wt_dealt")
+        ws_dealt = sb([P, 2, PACK, P], U8, "ws_dealt")
+
+        def deal_words():
+            nc.vector.tensor_copy(
+                out=wx_dealt[:].bitcast(I32).rearrange("p t (c i) -> p c t i", i=PACK),
+                in_=wx_raw[:].bitcast(I32).rearrange("p (c i t) -> p c t i", i=PACK, t=PACK),
+            )
+            nc.vector.tensor_copy(
+                out=wt_dealt[:].rearrange("p a t (m e) -> p a t m e", e=2),
+                in_=wt_raw[:].rearrange("p a (m t e) -> p a t m e", t=PACK, e=2),
+            )
+
+        def deal_scales():
+            nc.vector.tensor_copy(out=ws_dealt[:], in_=ws_raw[:].rearrange("p a (m t) -> p a t m", t=PACK))
+
+        tiers = {}
+
+        def two_tiers(quarter, engine):
+            words = sb([P, PACK * QUARTER], BF16, "cq_words_%d" % quarter, tag="id_words" if quarter == 0 else None)
+            interleave(engine, words[:], c_sb[quarter][:])
+            cq_codes, cq_scales = quantize(words[:], "cq_%d" % quarter)
+            rest = sb([P, PACK * QUARTER], BF16, "cr_words_%d" % quarter)
+            for s in range(QUARTER // SUB):
+                cols = slice(s * SUB, (s + 1) * SUB)
+                step = quarter * (QUARTER // SUB) + s
+                back = bank(step, [P, PACK, SUB], "back_%d" % step)
+                for t in range(PACK):
+                    nc.tensor.matmul_mx(
+                        out=back[:, t, :],
+                        lhsT=id_codes[:, t * P : (t + 1) * P].bitcast(FP8X4),
+                        lhsT_scale=id_scales[:, t * P : (t + 1) * P],
+                        rhs=cq_codes[:, cols].bitcast(FP8X4),
+                        rhs_scale=cq_scales[:, cols],
+                        start=True,
+                        stop=True,
+                    )
+                nc.vector.tensor_tensor(
+                    out=walk_words(rest[:, PACK * s * SUB : PACK * (s + 1) * SUB]),
+                    in0=walk_rows(c_sb[quarter][:, :, cols]),
+                    in1=walk_rows(back[:]),
+                    op=SUBTRACT,
+                )
+            tiers[quarter] = ((cq_codes, cq_scales), quantize(rest[:], "cr_%d" % quarter))
+
+        picked = {}
+        reuse = {(0, 0): "c_2", (0, 1): "c_3", (1, 1): "wgt_0"}
+
+        def gather(plane, j0, width):
+            a, i = divmod(plane, PACK)
+            half = j0 // HALF
+            if (a, half) not in picked:
+                picked[a, half] = sb([P, PACK, HALF], F32, "picked_%d_%d" % (a, half), tag=reuse.get((a, half)))
+            cols = slice(j0 - half * HALF, j0 - half * HALF + width)
+            nc.vector.tensor_tensor(
+                out=picked[a, half][:, i, cols],
+                in0=x_sb[plane][:].indirect(offsets[:, j0 // 16 : (j0 + width) // 16]),
+                in1=wgt_sb[half][:, cols],
+                op=MULT,
+            )
+
+        acc = {}
+
+        def acc_slice(ch, t):
+            j0, width = CHUNKS[ch]
+            per_bank = BANK // width
+            if (ch, t // per_bank) not in acc:
+                index = j0 // SUB + t // per_bank
+                acc[ch, t // per_bank] = bank(index, [P, per_bank, width], "acc_%d" % index)
+            return acc[ch, t // per_bank][:, t % per_bank, :]
+
+        def c_passes(ch):
+            j0, width = CHUNKS[ch]
+            per_bank = BANK // width
+            cols = slice(j0 % QUARTER, j0 % QUARTER + width)
+            for tier in range(2):
+                codes, scales = tiers[j0 // QUARTER][tier]
+                for t in range(PACK):
+                    nc.tensor.matmul_mx(
+                        out=acc_slice(ch, t),
+                        lhsT=wx_dealt[:, t, :].bitcast(FP8X4),
+                        lhsT_scale=ws_dealt[4:P, 0, t, :],
+                        rhs=codes[:, cols].bitcast(FP8X4),
+                        rhs_scale=scales[:, cols],
+                        start=(tier == 0 and t % per_bank == 0),
+                        stop=False,
+                    )
+
+        def x_passes(ch, a, codes, scales, col0):
+            width = CHUNKS[ch][1]
+            per_bank = BANK // width
+            for t in range(PACK):
+                for s in range(width // SUB):
+                    cols = slice(col0 + s * SUB, col0 + (s + 1) * SUB)
+                    nc.tensor.matmul_mx(
+                        out=acc_slice(ch, t)[:, s * SUB : (s + 1) * SUB],
+                        lhsT=wt_dealt[:, a, t, :].bitcast(FP4X4),
+                        lhsT_scale=ws_dealt[:, a, t, :],
+                        rhs=codes[:, cols].bitcast(FP8X4),
+                        rhs_scale=scales[:, cols],
+                        start=False,
+                        stop=(a == 1 and t % per_bank == per_bank - 1 and s == width // SUB - 1),
+                    )
+
+        def first_pass(half):
+            words = sb([P, PACK * HALF], BF16, "xg0_words_%d" % half)
+            interleave("scalar", words[:], picked[0, half][:])
+            codes, scales = quantize(words[:], "xg0_%d" % half)
+            for ch, (j0, width) in enumerate(CHUNKS):
+                if j0 // HALF == half:
+                    x_passes(ch, 0, codes, scales, j0 % HALF)
+
+        def second_pass(ch, engine):
+            j0, width = CHUNKS[ch]
+            words = sb([P, PACK * width], BF16, "xg1_words_%d" % ch)
+            interleave(engine, words[:], picked[1, j0 // HALF][:, :, j0 % HALF : j0 % HALF + width])
+            codes, scales = quantize(words[:], "xg1_%d" % ch)
+            x_passes(ch, 1, codes, scales, 0)
+
+        out_rows = out_0.rearrange("(p t) j -> p t j", t=PACK)
+        out_words = out_1[0].rearrange("p j i -> p (j i)")
+        out_scales = sb([P, J], U8, "out_scales")
+        results = {}
+
+        def activate(ch):
+            j0, width = CHUNKS[ch]
+            result = sb([P, PACK, width], F32, "result_%d" % ch)
+            for t in range(PACK):
+                nc.scalar.activation(out=result[:, t, :], in_=acc_slice(ch, t), func=GELU, bias=bias[:, t : t + 1])
+            nc.sync.dma_start(out=out_rows[:, :, j0 : j0 + width], in_=result[:])
+            results[ch] = result
+
+        def hand_on(ch, engine):
+            j0, width = CHUNKS[ch]
+            words = sb([P, PACK * width], BF16, "out_words_%d" % ch)
+            interleave(engine, words[:], results[ch][:])
+            codes = sb([P, width], U32, "out_codes_%d" % ch)
+            nc.vector.quantize_mx(out=codes[:].bitcast(FP8X4), scales=out_scales[:, j0 : j0 + width], in_=words[:])
+            nc.sync.dma_start(
+                out=out_words[:, PACK * j0 : PACK * (j0 + width)].bitcast(I32), in_=codes[:].bitcast(I32)
+            )
+
+        deal_words()
+        two_tiers(0, "vector")
+        for quarter in range(1, 4):
+            two_tiers(quarter, "scalar")
+        for plane in range(4):
+            gather(plane, 0, HALF)
+            gather(plane, HALF, HALF)
+        deal_scales()
+        for ch in range(len(CHUNKS)):
+            c_passes(ch)
+        first_pass(0)
+        first_pass(1)
+        for plane in range(4, 7):
+            gather(plane, 0, HALF)
+        gather(7, 0, QUARTER)
+        gather(7, QUARTER, QUARTER)
+        second_pass(0, "scalar")
+        second_pass(1, "scalar")
+        activate(0)
+        activate(1)
+        for plane in range(4, 8):
+            gather(plane, 512, 256)
+        second_pass(2, "scalar")
+        hand_on(0, "scalar")
+        activate(2)
+        for plane in range(4, 7):
+            gather(plane, 768, 256)
+        gather(7, 768, 128)
+        gather(7, 896, 128)
+        second_pass(3, "vector")
+        second_pass(4, "vector")
+        hand_on(1, "vector")
+        activate(3)
+        activate(4)
+        hand_on(2, "vector")
+        hand_on(3, "vector")
+        hand_on(4, "vector")
+        for q in range(4):
+            queue = nc.sync if q % 2 == 0 else nc.scalar
+            queue.dma_start(
+                out=out_2[0, 4 * q : 4 * q + 4, :].bitcast(I32), in_=out_scales[32 * q : 32 * q + 4, :].bitcast(I32)
+            )

@@ -15,6 +15,7 @@ FP8X4 = mybir.dt.float8_e4m3fn_x4
 FP4X4 = mybir.dt.float4_e2m1fn_x4
 MULT = mybir.AluOpType.mult
 SUBTRACT = mybir.AluOpType.subtract
+ADD = mybir.AluOpType.add
 IS_EQUAL = mybir.AluOpType.is_equal
 GELU = mybir.ActivationFunctionType.Gelu_apprx_tanh
 
@@ -24,15 +25,17 @@ BANK = 512
 HALF = 512
 QUARTER = 256
 SUB = 128
+ID_ROW = PACK * P + 1
+STEP = 2
 CHUNKS = [(0, 256), (256, 256), (512, 256), (768, 128), (896, 128)]
 
 
 def walk_rows(ap):
-    return ap.rearrange("p t (c i) -> p c t i", i=PACK)
+    return ap.rearrange("p t (c i) -> p c t i", i=STEP)
 
 
 def walk_words(ap):
-    return ap.rearrange("p (c i t) -> p c t i", i=PACK, t=PACK)
+    return ap.rearrange("p (c i t) -> p c t i", i=STEP, t=PACK)
 
 
 def tile_list_geluP_kernel(
@@ -66,10 +69,8 @@ def tile_list_geluP_kernel(
         offsets = keep.tile([P, J // 16], U16, name="offsets")
         nc.sync.dma_start(offsets[:], offs)
 
-        distance = sb([P, P], I32, "distance")
-        nc.gpsimd.iota(distance[:], pattern=[[1, P]], base=0, channel_multiplier=-1)
         ws_raw = sb([P, 2, N], U8, "ws_raw")
-        nc.gpsimd.memset(ws_raw[:].bitcast(I32), 0)
+        nc.vector.memset(ws_raw[:].bitcast(I32), 0)
 
         warm = sb([P, 8], F32, "warm")
         nc.vector.memset(warm[:], 0.0)
@@ -118,9 +119,11 @@ def tile_list_geluP_kernel(
         def load_bias():
             nc.sync.dma_start(out=bias[:], in_=b.rearrange("(p t) -> p t", t=PACK))
 
+        load_c(0)
+        load_c(1)
         load_weights()
-        for quarter in range(4):
-            load_c(quarter)
+        load_c(2)
+        load_c(3)
         load_wgt(0)
         load_x(0)
         load_wgt(1)
@@ -131,11 +134,24 @@ def tile_list_geluP_kernel(
         for plane in range(5, 8):
             load_x(plane)
 
-        id_words = sb([P, PACK, P, PACK], BF16, "id_words")
+        ones = sb([P, 32], F32, "ones")
+        nc.vector.memset(ones[:], 1.0)
+        column = sb([P, 32], F32, "column")
+        nc.vector.tensor_tensor_scan(out=column[:], data0=ones[:], data1=ones[:], initial=0.0, op0=MULT, op1=ADD)
+        id_words = sb([P, PACK * ID_ROW], BF16, "id_words")
         nc.vector.memset(id_words[:], 0.0)
-        for t in range(PACK):
-            nc.vector.tensor_single_scalar(out=id_words[:, t, :, t], in_=distance[:], scalar=0.0, op=IS_EQUAL)
-        id_codes, id_scales = quantize(id_words[:].rearrange("p t m i -> p (t m i)"), "id")
+        row = sb([P, 32], F32, "row")
+        nc.vector.transpose(out=row[:], in_=column[:])
+        diagonal = sb([P, 32], F32, "diagonal")
+        nc.vector.tensor_tensor(out=diagonal[:], in0=column[:], in1=row[:], op=IS_EQUAL)
+        id_view = id_words[:].rearrange("p (t r) -> p t r", t=PACK)
+        for q in range(4):
+            rows = slice(32 * q, 32 * q + 32)
+            nc.vector.tensor_copy(
+                out=id_view[rows, :, P * q : P * (q + 1) : PACK],
+                in_=diagonal[rows, :].unsqueeze(1).to_broadcast([32, PACK, 32]),
+            )
+        id_codes, id_scales = quantize(id_words[:, 0 : PACK * PACK * P], "id")
 
         wx_dealt = sb([P, PACK, P], U32, "wx_dealt")
         wt_dealt = sb([P, 2, PACK, 2 * P], U8, "wt_dealt")
@@ -157,7 +173,7 @@ def tile_list_geluP_kernel(
         tiers = {}
 
         def two_tiers(quarter, engine):
-            words = sb([P, PACK * QUARTER], BF16, "cq_words_%d" % quarter, tag="id_words" if quarter == 0 else None)
+            words = sb([P, PACK * QUARTER], BF16, "cq_words_%d" % quarter)
             interleave(engine, words[:], c_sb[quarter][:])
             cq_codes, cq_scales = quantize(words[:], "cq_%d" % quarter)
             rest = sb([P, PACK * QUARTER], BF16, "cr_words_%d" % quarter)
@@ -280,10 +296,11 @@ def tile_list_geluP_kernel(
                 out=out_words[:, PACK * j0 : PACK * (j0 + width)].bitcast(I32), in_=codes[:].bitcast(I32)
             )
 
-        deal_words()
         two_tiers(0, "vector")
-        for quarter in range(1, 4):
-            two_tiers(quarter, "scalar")
+        two_tiers(1, "scalar")
+        deal_words()
+        two_tiers(2, "scalar")
+        two_tiers(3, "scalar")
         for plane in range(4):
             gather(plane, 0, HALF)
             gather(plane, HALF, HALF)
@@ -311,7 +328,7 @@ def tile_list_geluP_kernel(
         gather(7, 896, 128)
         second_pass(3, "vector")
         second_pass(4, "vector")
-        hand_on(1, "vector")
+        hand_on(1, "scalar")
         activate(3)
         activate(4)
         hand_on(2, "vector")

@@ -1,6 +1,7 @@
 from contextlib import ExitStack
 
 import concourse.mybir as mybir
+from concourse.masks import make_identity
 
 K, L, N, T, J = 1024, 512, 512, 2048, 1024
 FLOPS = 2 * N * J * (K + 3 * L)
@@ -17,6 +18,7 @@ MULT = mybir.AluOpType.mult
 SUBTRACT = mybir.AluOpType.subtract
 ADD = mybir.AluOpType.add
 IS_EQUAL = mybir.AluOpType.is_equal
+COPY = mybir.ActivationFunctionType.Copy
 GELU = mybir.ActivationFunctionType.Gelu_apprx_tanh
 
 P = 128
@@ -59,9 +61,9 @@ def tile_list_geluP_kernel(
             else:
                 nc.scalar.copy(out=walk_words(words), in_=walk_rows(rows))
 
-        def quantize(words, name):
+        def quantize(words, name, tag=None):
             width = words.shape[1] // PACK
-            codes = sb([P, width], U32, name + "_codes")
+            codes = sb([P, width], U32, name + "_codes", tag=tag)
             scales = sb([P, width], U8, name + "_scales")
             nc.vector.quantize_mx(out=codes[:].bitcast(FP8X4), scales=scales[:], in_=words)
             return codes, scales
@@ -71,6 +73,11 @@ def tile_list_geluP_kernel(
 
         ws_raw = sb([P, 2, N], U8, "ws_raw")
         nc.vector.memset(ws_raw[:].bitcast(I32), 0)
+
+        id_words = sb([P, PACK * ID_ROW], BF16, "id_words")
+        nc.gpsimd.memset(id_words[:], 0.0)
+        ident = sb([P, P], F32, "ident")
+        make_identity(nc, ident[:])
 
         warm = sb([P, 8], F32, "warm")
         nc.vector.memset(warm[:], 0.0)
@@ -127,19 +134,20 @@ def tile_list_geluP_kernel(
         load_wgt(0)
         load_x(0)
         load_wgt(1)
-        for plane in range(1, 5):
-            load_scales(plane - 1)
-            load_x(plane)
+        load_scales(0)
+        load_scales(1)
+        load_x(1)
+        load_scales(2)
+        load_scales(3)
+        load_x(2)
         load_bias()
-        for plane in range(5, 8):
+        for plane in range(3, 8):
             load_x(plane)
 
         ones = sb([P, 32], F32, "ones")
         nc.vector.memset(ones[:], 1.0)
         column = sb([P, 32], F32, "column")
         nc.vector.tensor_tensor_scan(out=column[:], data0=ones[:], data1=ones[:], initial=0.0, op0=MULT, op1=ADD)
-        id_words = sb([P, PACK * ID_ROW], BF16, "id_words")
-        nc.vector.memset(id_words[:], 0.0)
         row = sb([P, 32], F32, "row")
         nc.vector.transpose(out=row[:], in_=column[:])
         diagonal = sb([P, 32], F32, "diagonal")
@@ -153,65 +161,115 @@ def tile_list_geluP_kernel(
             )
         id_codes, id_scales = quantize(id_words[:, 0 : PACK * PACK * P], "id")
 
-        wx_dealt = sb([P, PACK, P], U32, "wx_dealt")
-        wt_dealt = sb([P, 2, PACK, 2 * P], U8, "wt_dealt")
-        ws_dealt = sb([P, 2, PACK, P], U8, "ws_dealt")
+        dealt = {}
 
         def deal_words():
+            wx_dealt = sb([P, PACK, P], U32, "wx_dealt", tag="cq_words_0")
+            wt_dealt = sb([P, 2, PACK, 2 * P], U8, "wt_dealt", tag="cq_words_1")
+            dealt["wx"] = wx_dealt
+            dealt["wt"] = wt_dealt
             nc.vector.tensor_copy(
                 out=wx_dealt[:].bitcast(I32).rearrange("p t (c i) -> p c t i", i=PACK),
                 in_=wx_raw[:].bitcast(I32).rearrange("p (c i t) -> p c t i", i=PACK, t=PACK),
             )
             nc.vector.tensor_copy(
-                out=wt_dealt[:].rearrange("p a t (m e) -> p a t m e", e=2),
-                in_=wt_raw[:].rearrange("p a (m t e) -> p a t m e", t=PACK, e=2),
+                out=wt_dealt[:].bitcast(U16),
+                in_=wt_raw[:].bitcast(U16).rearrange("p a (m t) -> p a t m", t=PACK),
             )
 
         def deal_scales():
+            ws_dealt = sb([P, 2, PACK, P], U8, "ws_dealt", tag="x_1")
+            dealt["ws"] = ws_dealt
             nc.vector.tensor_copy(out=ws_dealt[:], in_=ws_raw[:].rearrange("p a (m t) -> p a t m", t=PACK))
 
         tiers = {}
+        rests = {}
 
-        def two_tiers(quarter, engine):
+        def first_tier(quarter, engine):
             words = sb([P, PACK * QUARTER], BF16, "cq_words_%d" % quarter)
             interleave(engine, words[:], c_sb[quarter][:])
-            cq_codes, cq_scales = quantize(words[:], "cq_%d" % quarter)
+            tiers[quarter, 0] = quantize(words[:], "cq_%d" % quarter)
+
+        def values_back(quarter, s, index):
+            cq_codes, cq_scales = tiers[quarter, 0]
+            cols = slice(s * SUB, (s + 1) * SUB)
+            back = bank(index, [P, PACK, SUB], "back_%d_%d" % (quarter, s))
+            for t in range(PACK):
+                nc.tensor.matmul_mx(
+                    out=back[:, t, :],
+                    lhsT=id_codes[:, t * P : (t + 1) * P].bitcast(FP8X4),
+                    lhsT_scale=id_scales[:, t * P : (t + 1) * P],
+                    rhs=cq_codes[:, cols].bitcast(FP8X4),
+                    rhs_scale=cq_scales[:, cols],
+                    start=True,
+                    stop=True,
+                )
+            return back
+
+        def second_tier_on_vector(quarter):
             rest = sb([P, PACK * QUARTER], BF16, "cr_words_%d" % quarter)
             for s in range(QUARTER // SUB):
-                cols = slice(s * SUB, (s + 1) * SUB)
-                step = quarter * (QUARTER // SUB) + s
-                back = bank(step, [P, PACK, SUB], "back_%d" % step)
-                for t in range(PACK):
-                    nc.tensor.matmul_mx(
-                        out=back[:, t, :],
-                        lhsT=id_codes[:, t * P : (t + 1) * P].bitcast(FP8X4),
-                        lhsT_scale=id_scales[:, t * P : (t + 1) * P],
-                        rhs=cq_codes[:, cols].bitcast(FP8X4),
-                        rhs_scale=cq_scales[:, cols],
-                        start=True,
-                        stop=True,
-                    )
+                back = values_back(quarter, s, 2 * quarter + s)
                 nc.vector.tensor_tensor(
                     out=walk_words(rest[:, PACK * s * SUB : PACK * (s + 1) * SUB]),
-                    in0=walk_rows(c_sb[quarter][:, :, cols]),
+                    in0=walk_rows(c_sb[quarter][:, :, s * SUB : (s + 1) * SUB]),
                     in1=walk_rows(back[:]),
                     op=SUBTRACT,
                 )
-            tiers[quarter] = ((cq_codes, cq_scales), quantize(rest[:], "cr_%d" % quarter))
+            tiers[quarter, 1] = quantize(rest[:], "cr_%d" % quarter)
+
+        def second_tier_on_tensor(quarter):
+            turned = []
+            for s in range(QUARTER // SUB):
+                back = values_back(quarter, s, 6 + s)
+                negated = sb([P, PACK, SUB], F32, "negated_%d_%d" % (quarter, s))
+                nc.scalar.activation(out=negated[:], in_=back[:], func=COPY, scale=-1.0)
+                left = bank(4 + s, [P, PACK, P], "left_%d_%d" % (quarter, s))
+                for t in range(PACK):
+                    nc.tensor.matmul(
+                        left[:, t, :], c_sb[quarter][:, t, s * SUB : (s + 1) * SUB], ident[:],
+                        start=True, stop=False, is_transpose=True,
+                    )
+                    nc.tensor.matmul(
+                        left[:, t, :], negated[:, t, :], ident[:], start=False, stop=True, is_transpose=True
+                    )
+                pairs = sb([P, PACK * P], BF16, "pairs_%d_%d" % (quarter, s))
+                nc.scalar.copy(
+                    out=pairs[:].rearrange("j (u p e) -> j u p e", u=2, e=2),
+                    in_=left[:].rearrange("j (u e) p -> j u p e", u=2),
+                )
+                turned.append(pairs)
+            again = bank(3, [P, 2, 2, SUB], "again_%d" % quarter)
+            for s in range(QUARTER // SUB):
+                for u in range(2):
+                    nc.tensor.transpose(again[:, s, u, :], turned[s][:].bitcast(F32)[:, u * P : (u + 1) * P], ident[:])
+            rest = sb([P, PACK * QUARTER], BF16, "cr_words_%d" % quarter)
+            nc.scalar.copy(
+                out=rest[:].bitcast(F32).rearrange("p (s j u) -> p s j u", s=2, u=2),
+                in_=again[:].rearrange("p s u j -> p s j u"),
+            )
+            rests[quarter] = rest
+
+        def quantize_rest(quarter, tag):
+            tiers[quarter, 1] = quantize(rests[quarter][:], "cr_%d" % quarter, tag)
 
         picked = {}
-        reuse = {(0, 0): "c_2", (0, 1): "c_3", (1, 1): "wgt_0"}
+
+        def stage(a, j0, width, tag=None):
+            tile = sb([P, PACK, width], F32, "picked_%d_%d" % (a, j0), tag=tag)
+            for j in range(j0, j0 + width, SUB):
+                picked[a, j] = (tile, j0)
+
+        def picked_cols(a, j0, width):
+            tile, base = picked[a, j0]
+            return tile[:, :, j0 - base : j0 - base + width]
 
         def gather(plane, j0, width):
             a, i = divmod(plane, PACK)
-            half = j0 // HALF
-            if (a, half) not in picked:
-                picked[a, half] = sb([P, PACK, HALF], F32, "picked_%d_%d" % (a, half), tag=reuse.get((a, half)))
-            cols = slice(j0 - half * HALF, j0 - half * HALF + width)
             nc.vector.tensor_tensor(
-                out=picked[a, half][:, i, cols],
+                out=picked_cols(a, j0, width)[:, i, :],
                 in0=x_sb[plane][:].indirect(offsets[:, j0 // 16 : (j0 + width) // 16]),
-                in1=wgt_sb[half][:, cols],
+                in1=wgt_sb[j0 // HALF][:, j0 % HALF : j0 % HALF + width],
                 op=MULT,
             )
 
@@ -230,12 +288,12 @@ def tile_list_geluP_kernel(
             per_bank = BANK // width
             cols = slice(j0 % QUARTER, j0 % QUARTER + width)
             for tier in range(2):
-                codes, scales = tiers[j0 // QUARTER][tier]
+                codes, scales = tiers[j0 // QUARTER, tier]
                 for t in range(PACK):
                     nc.tensor.matmul_mx(
                         out=acc_slice(ch, t),
-                        lhsT=wx_dealt[:, t, :].bitcast(FP8X4),
-                        lhsT_scale=ws_dealt[4:P, 0, t, :],
+                        lhsT=dealt["wx"][:, t, :].bitcast(FP8X4),
+                        lhsT_scale=dealt["ws"][4:P, 0, t, :],
                         rhs=codes[:, cols].bitcast(FP8X4),
                         rhs_scale=scales[:, cols],
                         start=(tier == 0 and t % per_bank == 0),
@@ -250,8 +308,8 @@ def tile_list_geluP_kernel(
                     cols = slice(col0 + s * SUB, col0 + (s + 1) * SUB)
                     nc.tensor.matmul_mx(
                         out=acc_slice(ch, t)[:, s * SUB : (s + 1) * SUB],
-                        lhsT=wt_dealt[:, a, t, :].bitcast(FP4X4),
-                        lhsT_scale=ws_dealt[:, a, t, :],
+                        lhsT=dealt["wt"][:, a, t, :].bitcast(FP4X4),
+                        lhsT_scale=dealt["ws"][:, a, t, :],
                         rhs=codes[:, cols].bitcast(FP8X4),
                         rhs_scale=scales[:, cols],
                         start=False,
@@ -260,7 +318,7 @@ def tile_list_geluP_kernel(
 
         def first_pass(half):
             words = sb([P, PACK * HALF], BF16, "xg0_words_%d" % half)
-            interleave("scalar", words[:], picked[0, half][:])
+            interleave("scalar", words[:], picked_cols(0, half * HALF, HALF))
             codes, scales = quantize(words[:], "xg0_%d" % half)
             for ch, (j0, width) in enumerate(CHUNKS):
                 if j0 // HALF == half:
@@ -269,7 +327,7 @@ def tile_list_geluP_kernel(
         def second_pass(ch, engine):
             j0, width = CHUNKS[ch]
             words = sb([P, PACK * width], BF16, "xg1_words_%d" % ch)
-            interleave(engine, words[:], picked[1, j0 // HALF][:, :, j0 % HALF : j0 % HALF + width])
+            interleave(engine, words[:], picked_cols(1, j0, width))
             codes, scales = quantize(words[:], "xg1_%d" % ch)
             x_passes(ch, 1, codes, scales, 0)
 
@@ -296,19 +354,30 @@ def tile_list_geluP_kernel(
                 out=out_words[:, PACK * j0 : PACK * (j0 + width)].bitcast(I32), in_=codes[:].bitcast(I32)
             )
 
-        two_tiers(0, "vector")
-        two_tiers(1, "scalar")
+        for quarter in range(2):
+            first_tier(quarter, "scalar")
+        for quarter in range(2):
+            second_tier_on_vector(quarter)
+        for quarter in range(2, 4):
+            first_tier(quarter, "scalar")
         deal_words()
-        two_tiers(2, "scalar")
-        two_tiers(3, "scalar")
-        for plane in range(4):
+        for quarter in range(2, 4):
+            second_tier_on_tensor(quarter)
+        stage(0, 0, HALF, "c_0")
+        stage(0, HALF, HALF, "c_1")
+        for plane in range(2):
             gather(plane, 0, HALF)
             gather(plane, HALF, HALF)
         deal_scales()
+        for plane in range(2, 4):
+            gather(plane, 0, HALF)
+            gather(plane, HALF, HALF)
+            quantize_rest(plane, "x_%d" % plane)
         for ch in range(len(CHUNKS)):
             c_passes(ch)
         first_pass(0)
         first_pass(1)
+        stage(1, 0, HALF)
         for plane in range(4, 7):
             gather(plane, 0, HALF)
         gather(7, 0, QUARTER)
@@ -317,6 +386,7 @@ def tile_list_geluP_kernel(
         second_pass(1, "scalar")
         activate(0)
         activate(1)
+        stage(1, HALF, HALF, "wgt_0")
         for plane in range(4, 8):
             gather(plane, 512, 256)
         second_pass(2, "scalar")

@@ -79,11 +79,6 @@ def tile_list_geluP_kernel(
         ident = sb([P, P], F32, "ident")
         make_identity(nc, ident[:])
 
-        warm = sb([P, 8], F32, "warm")
-        nc.vector.memset(warm[:], 0.0)
-        warm2 = sb([P, 8], F32, "warm2")
-        nc.scalar.activation(out=warm2[:], in_=warm[:], func=GELU)
-
         wx_raw = sb([P, N], U32, "wx_raw")
         wt_raw = sb([P, 2, 2 * N], U8, "wt_raw")
         bias = sb([P, PACK], F32, "bias")
@@ -118,10 +113,12 @@ def tile_list_geluP_kernel(
             nc.sync.dma_start(out=tile[:], in_=x_rows[plane // PACK, plane % PACK])
             x_sb[plane] = tile
 
+        shared = sb([P, 2 * PACK * QUARTER], F32, "shared")
+        wgt_sb[0] = shared[:, 0:HALF]
+        wgt_sb[1] = sb([P, HALF], F32, "wgt_1")[:]
+
         def load_wgt(half):
-            tile = sb([P, HALF], F32, "wgt_%d" % half)
-            nc.sync.dma_start(out=tile[:], in_=wgt[:, half * HALF : (half + 1) * HALF])
-            wgt_sb[half] = tile
+            nc.sync.dma_start(out=wgt_sb[half], in_=wgt[:, half * HALF : (half + 1) * HALF])
 
         def load_bias():
             nc.sync.dma_start(out=bias[:], in_=b.rearrange("(p t) -> p t", t=PACK))
@@ -260,6 +257,12 @@ def tile_list_geluP_kernel(
             for j in range(j0, j0 + width, SUB):
                 picked[a, j] = (tile, j0)
 
+        def stage_shared(j0):
+            first = PACK * (j0 - HALF)
+            rows = shared[:, first : first + PACK * QUARTER].rearrange("p (t j) -> p t j", t=PACK)
+            for j in range(j0, j0 + QUARTER, SUB):
+                picked[1, j] = (rows, j0)
+
         def picked_cols(a, j0, width):
             tile, base = picked[a, j0]
             return tile[:, :, j0 - base : j0 - base + width]
@@ -326,9 +329,12 @@ def tile_list_geluP_kernel(
 
         def second_pass(ch, engine):
             j0, width = CHUNKS[ch]
-            words = sb([P, PACK * width], BF16, "xg1_words_%d" % ch)
-            interleave(engine, words[:], picked_cols(1, j0, width))
-            codes, scales = quantize(words[:], "xg1_%d" % ch)
+            if width == QUARTER:
+                words = shared[:, (ch + 1) * HALF : (ch + 2) * HALF].bitcast(BF16)
+            else:
+                words = sb([P, PACK * width], BF16, "xg1_words_%d" % ch)[:]
+            interleave(engine, words, picked_cols(1, j0, width))
+            codes, scales = quantize(words, "xg1_%d" % ch)
             x_passes(ch, 1, codes, scales, 0)
 
         out_rows = out_0.rearrange("(p t) j -> p t j", t=PACK)
@@ -384,20 +390,21 @@ def tile_list_geluP_kernel(
         gather(7, QUARTER, QUARTER)
         second_pass(0, "scalar")
         second_pass(1, "scalar")
-        activate(0)
-        activate(1)
-        stage(1, HALF, HALF, "wgt_0")
+        stage_shared(512)
+        stage_shared(768)
         for plane in range(4, 8):
             gather(plane, 512, 256)
-        second_pass(2, "scalar")
-        hand_on(0, "scalar")
-        activate(2)
+        second_pass(2, "vector")
+        activate(0)
+        activate(1)
         for plane in range(4, 7):
             gather(plane, 768, 256)
         gather(7, 768, 128)
         gather(7, 896, 128)
         second_pass(3, "vector")
         second_pass(4, "vector")
+        hand_on(0, "scalar")
+        activate(2)
         hand_on(1, "scalar")
         activate(3)
         activate(4)

from contextlib import ExitStack

import concourse.mybir as mybir
from concourse.masks import make_identity

K, L, N, T, J = 1024, 512, 512, 2048, 1024
FLOPS = 2 * N * J * (K + 3 * L)

F32 = mybir.dt.float32
BF16 = mybir.dt.bfloat16
I32 = mybir.dt.int32
U32 = mybir.dt.uint32
U16 = mybir.dt.uint16
U8 = mybir.dt.uint8
FP8X4 = mybir.dt.float8_e4m3fn_x4
FP4X4 = mybir.dt.float4_e2m1fn_x4
MULT = mybir.AluOpType.mult
SUBTRACT = mybir.AluOpType.subtract
ADD = mybir.AluOpType.add
IS_EQUAL = mybir.AluOpType.is_equal
COPY = mybir.ActivationFunctionType.Copy
GELU = mybir.ActivationFunctionType.Gelu_apprx_tanh

P = 128
PACK = 4
BANK = 512
HALF = 512
QUARTER = 256
SUB = 128
ID_ROW = PACK * P + 1
STEP = 2
CHUNKS = [(0, 256), (256, 256), (512, 256), (768, 128), (896, 128)]


def walk_rows(ap):
    return ap.rearrange("p t (c i) -> p c t i", i=STEP)


def walk_words(ap):
    return ap.rearrange("p (c i t) -> p c t i", i=STEP, t=PACK)


def tile_list_geluP_kernel(
    tc, xT, wgt, wt_words, wt_scales, c, wx_words, wx_scales, b, offs, out_0, out_1, out_2
):
    nc = tc.nc

    with ExitStack() as ctx:
        keep = ctx.enter_context(tc.tile_pool(name="keep", bufs=1))
        psum = ctx.enter_context(tc.psum_pool(name="psum", bufs=1))

        def sb(shape, dtype, name, tag=None):
            return keep.tile(shape, dtype, name=name, tag=tag or name, align_bytes=64)

        def bank(index, shape, name):
            return psum.tile(shape, F32, name=name, tag="bank%d" % index)

        def interleave(engine, words, rows):
            if engine == "vector":
                nc.vector.tensor_copy(out=walk_words(words), in_=walk_rows(rows))
            else:
                nc.scalar.copy(out=walk_words(words), in_=walk_rows(rows))

        def quantize(words, name, tag=None):
            width = words.shape[1] // PACK
            codes = sb([P, width], U32, name + "_codes", tag=tag)
            scales = sb([P, width], U8, name + "_scales")
            nc.vector.quantize_mx(out=codes[:].bitcast(FP8X4), scales=scales[:], in_=words)
            return codes, scales

        offsets = keep.tile([P, J // 16], U16, name="offsets")
        nc.sync.dma_start(offsets[:], offs)

        ws_raw = sb([P, 2, N], U8, "ws_raw")
        nc.vector.memset(ws_raw[:].bitcast(I32), 0)

        id_words = sb([P, PACK * ID_ROW], BF16, "id_words")
        nc.gpsimd.memset(id_words[:], 0.0)
        ident = sb([P, P], F32, "ident")
        make_identity(nc, ident[:])

        wx_raw = sb([P, N], U32, "wx_raw")
        wt_raw = sb([P, 2, 2 * N], U8, "wt_raw")
        bias = sb([P, PACK], F32, "bias")

        def load_weights():
            nc.sync.dma_start(out=wx_raw[:].bitcast(I32), in_=wx_words[0].rearrange("p n i -> p (n i)").bitcast(I32))
            nc.sync.dma_start(out=wt_raw[:].bitcast(I32), in_=wt_words.rearrange("a p n -> p a n").bitcast(I32))

        def load_scales(q):
            nc.sync.dma_start(
                out=ws_raw[32 * q : 32 * q + 4, :, :].bitcast(I32),
                in_=wt_scales[:, 4 * q : 4 * q + 4, :].rearrange("a r n -> r a n").bitcast(I32),
            )
            nc.sync.dma_start(
                out=ws_raw[32 * q + 4 : 32 * q + 8, 0, :].bitcast(I32),
                in_=wx_scales[0, 4 * q : 4 * q + 4, :].bitcast(I32),
            )

        c_rows = c.rearrange("(p t) j -> p t j", t=PACK)
        x_rows = xT.rearrange("(a p i) t -> a i p t", a=2, i=PACK)
        c_sb = {}
        x_sb = {}
        wgt_sb = {}

        def load_c(quarter):
            tile = sb([P, PACK, QUARTER], F32, "c_%d" % quarter)
            nc.sync.dma_start(out=tile[:], in_=c_rows[:, :, quarter * QUARTER : (quarter + 1) * QUARTER])
            c_sb[quarter] = tile

        def load_x(plane):
            tile = sb([P, T], F32, "x_%d" % plane)
            nc.sync.dma_start(out=tile[:], in_=x_rows[plane // PACK, plane % PACK])
            x_sb[plane] = tile

        shared = sb([P, 2 * PACK * QUARTER], F32, "shared")
        wgt_sb[0] = shared[:, 0:HALF]
        wgt_sb[1] = sb([P, HALF], F32, "wgt_1")[:]

        def load_wgt(half):
            nc.sync.dma_start(out=wgt_sb[half], in_=wgt[:, half * HALF : (half + 1) * HALF])

        def load_bias():
            nc.sync.dma_start(out=bias[:], in_=b.rearrange("(p t) -> p t", t=PACK))

        load_c(0)
        load_c(1)
        load_weights()
        load_c(2)
        load_c(3)
        load_wgt(0)
        load_x(0)
        load_wgt(1)
        load_scales(0)
        load_scales(1)
        load_x(1)
        load_scales(2)
        load_scales(3)
        load_x(2)
        load_bias()
        for plane in range(3, 8):
            load_x(plane)

        ones = sb([P, 32], F32, "ones")
        nc.vector.memset(ones[:], 1.0)
        column = sb([P, 32], F32, "column")
        nc.vector.tensor_tensor_scan(out=column[:], data0=ones[:], data1=ones[:], initial=0.0, op0=MULT, op1=ADD)
        row = sb([P, 32], F32, "row")
        nc.vector.transpose(out=row[:], in_=column[:])
        diagonal = sb([P, 32], F32, "diagonal")
        nc.vector.tensor_tensor(out=diagonal[:], in0=column[:], in1=row[:], op=IS_EQUAL)
        id_view = id_words[:].rearrange("p (t r) -> p t r", t=PACK)
        for q in range(4):
            rows = slice(32 * q, 32 * q + 32)
            nc.vector.tensor_copy(
                out=id_view[rows, :, P * q : P * (q + 1) : PACK],
                in_=diagonal[rows, :].unsqueeze(1).to_broadcast([32, PACK, 32]),
            )
        id_codes, id_scales = quantize(id_words[:, 0 : PACK * PACK * P], "id")

        dealt = {}

        def deal_words():
            wx_dealt = sb([P, PACK, P], U32, "wx_dealt", tag="cq_words_0")
            wt_dealt = sb([P, 2, PACK, 2 * P], U8, "wt_dealt", tag="cq_words_1")
            dealt["wx"] = wx_dealt
            dealt["wt"] = wt_dealt
            nc.vector.tensor_copy(
                out=wx_dealt[:].bitcast(I32).rearrange("p t (c i) -> p c t i", i=PACK),
                in_=wx_raw[:].bitcast(I32).rearrange("p (c i t) -> p c t i", i=PACK, t=PACK),
            )
            nc.vector.tensor_copy(
                out=wt_dealt[:].bitcast(U16),
                in_=wt_raw[:].bitcast(U16).rearrange("p a (m t) -> p a t m", t=PACK),
            )

        def deal_scales():
            ws_dealt = sb([P, 2, PACK, P], U8, "ws_dealt", tag="x_1")
            dealt["ws"] = ws_dealt
            nc.vector.tensor_copy(out=ws_dealt[:], in_=ws_raw[:].rearrange("p a (m t) -> p a t m", t=PACK))

        tiers = {}
        rests = {}

        def first_tier(quarter, engine):
            words = sb([P, PACK * QUARTER], BF16, "cq_words_%d" % quarter)
            interleave(engine, words[:], c_sb[quarter][:])
            tiers[quarter, 0] = quantize(words[:], "cq_%d" % quarter)

        def values_back(quarter, s, index):
            cq_codes, cq_scales = tiers[quarter, 0]
            cols = slice(s * SUB, (s + 1) * SUB)
            back = bank(index, [P, PACK, SUB], "back_%d_%d" % (quarter, s))
            for t in range(PACK):
                nc.tensor.matmul_mx(
                    out=back[:, t, :],
                    lhsT=id_codes[:, t * P : (t + 1) * P].bitcast(FP8X4),
                    lhsT_scale=id_scales[:, t * P : (t + 1) * P],
                    rhs=cq_codes[:, cols].bitcast(FP8X4),
                    rhs_scale=cq_scales[:, cols],
                    start=True,
                    stop=True,
                )
            return back

        def second_tier_on_vector(quarter):
            rest = sb([P, PACK * QUARTER], BF16, "cr_words_%d" % quarter)
            for s in range(QUARTER // SUB):
                back = values_back(quarter, s, 2 * quarter + s)
                nc.vector.tensor_tensor(
                    out=walk_words(rest[:, PACK * s * SUB : PACK * (s + 1) * SUB]),
                    in0=walk_rows(c_sb[quarter][:, :, s * SUB : (s + 1) * SUB]),
                    in1=walk_rows(back[:]),
                    op=SUBTRACT,
                )
            tiers[quarter, 1] = quantize(rest[:], "cr_%d" % quarter)

        def second_tier_on_tensor(quarter):
            turned = []
            for s in range(QUARTER // SUB):
                back = values_back(quarter, s, 6 + s)
                negated = sb([P, PACK, SUB], F32, "negated_%d_%d" % (quarter, s))
                nc.scalar.activation(out=negated[:], in_=back[:], func=COPY, scale=-1.0)
                left = bank(4 + s, [P, PACK, P], "left_%d_%d" % (quarter, s))
                for t in range(PACK):
                    nc.tensor.matmul(
                        left[:, t, :], c_sb[quarter][:, t, s * SUB : (s + 1) * SUB], ident[:],
                        start=True, stop=False, is_transpose=True,
                    )
                    nc.tensor.matmul(
                        left[:, t, :], negated[:, t, :], ident[:], start=False, stop=True, is_transpose=True
                    )
                pairs = sb([P, PACK * P], BF16, "pairs_%d_%d" % (quarter, s))
                nc.scalar.copy(
                    out=pairs[:].rearrange("j (u p e) -> j u p e", u=2, e=2),
                    in_=left[:].rearrange("j (u e) p -> j u p e", u=2),
                )
                turned.append(pairs)
            again = bank(3, [P, 2, 2, SUB], "again_%d" % quarter)
            for s in range(QUARTER // SUB):
                for u in range(2):
                    nc.tensor.transpose(again[:, s, u, :], turned[s][:].bitcast(F32)[:, u * P : (u + 1) * P], ident[:])
            rest = sb([P, PACK * QUARTER], BF16, "cr_words_%d" % quarter)
            nc.scalar.copy(
                out=rest[:].bitcast(F32).rearrange("p (s j u) -> p s j u", s=2, u=2),
                in_=again[:].rearrange("p s u j -> p s j u"),
            )
            rests[quarter] = rest

        def quantize_rest(quarter, tag):
            tiers[quarter, 1] = quantize(rests[quarter][:], "cr_%d" % quarter, tag)

        picked = {}

        def stage(a, j0, width, tag=None):
            tile = sb([P, PACK, width], F32, "picked_%d_%d" % (a, j0), tag=tag)
            for j in range(j0, j0 + width, SUB):
                picked[a, j] = (tile, j0)

        def stage_shared(j0):
            first = PACK * (j0 - HALF)
            rows = shared[:, first : first + PACK * QUARTER].rearrange("p (t j) -> p t j", t=PACK)
            for j in range(j0, j0 + QUARTER, SUB):
                picked[1, j] = (rows, j0)

        def picked_cols(a, j0, width):
            tile, base = picked[a, j0]
            return tile[:, :, j0 - base : j0 - base + width]

        def gather(plane, j0, width):
            a, i = divmod(plane, PACK)
            nc.vector.tensor_tensor(
                out=picked_cols(a, j0, width)[:, i, :],
                in0=x_sb[plane][:].indirect(offsets[:, j0 // 16 : (j0 + width) // 16]),
                in1=wgt_sb[j0 // HALF][:, j0 % HALF : j0 % HALF + width],
                op=MULT,
            )

        acc = {}

        def acc_slice(ch, t):
            j0, width = CHUNKS[ch]
            per_bank = BANK // width
            if (ch, t // per_bank) not in acc:
                index = j0 // SUB + t // per_bank
                acc[ch, t // per_bank] = bank(index, [P, per_bank, width], "acc_%d" % index)
            return acc[ch, t // per_bank][:, t % per_bank, :]

        def c_passes(ch):
            j0, width = CHUNKS[ch]
            per_bank = BANK // width
            cols = slice(j0 % QUARTER, j0 % QUARTER + width)
            for tier in range(2):
                codes, scales = tiers[j0 // QUARTER, tier]
                for t in range(PACK):
                    nc.tensor.matmul_mx(
                        out=acc_slice(ch, t),
                        lhsT=dealt["wx"][:, t, :].bitcast(FP8X4),
                        lhsT_scale=dealt["ws"][4:P, 0, t, :],
                        rhs=codes[:, cols].bitcast(FP8X4),
                        rhs_scale=scales[:, cols],
                        start=(tier == 0 and t % per_bank == 0),
                        stop=False,
                    )

        def x_passes(ch, a, codes, scales, col0):
            width = CHUNKS[ch][1]
            per_bank = BANK // width
            for t in range(PACK):
                for s in range(width // SUB):
                    cols = slice(col0 + s * SUB, col0 + (s + 1) * SUB)
                    nc.tensor.matmul_mx(
                        out=acc_slice(ch, t)[:, s * SUB : (s + 1) * SUB],
                        lhsT=dealt["wt"][:, a, t, :].bitcast(FP4X4),
                        lhsT_scale=dealt["ws"][:, a, t, :],
                        rhs=codes[:, cols].bitcast(FP8X4),
                        rhs_scale=scales[:, cols],
                        start=False,
                        stop=(a == 1 and t % per_bank == per_bank - 1 and s == width // SUB - 1),
                    )

        def first_pass(half):
            words = sb([P, PACK * HALF], BF16, "xg0_words_%d" % half)
            interleave("scalar", words[:], picked_cols(0, half * HALF, HALF))
            codes, scales = quantize(words[:], "xg0_%d" % half)
            for ch, (j0, width) in enumerate(CHUNKS):
                if j0 // HALF == half:
                    x_passes(ch, 0, codes, scales, j0 % HALF)

        def second_pass(ch, engine):
            j0, width = CHUNKS[ch]
            if width == QUARTER:
                words = shared[:, (ch + 1) * HALF : (ch + 2) * HALF].bitcast(BF16)
            else:
                words = sb([P, PACK * width], BF16, "xg1_words_%d" % ch)[:]
            interleave(engine, words, picked_cols(1, j0, width))
            codes, scales = quantize(words, "xg1_%d" % ch)
            x_passes(ch, 1, codes, scales, 0)

        out_rows = out_0.rearrange("(p t) j -> p t j", t=PACK)
        out_words = out_1[0].rearrange("p j i -> p (j i)")
        out_scales = sb([P, J], U8, "out_scales")
        results = {}

        def activate(ch):
            j0, width = CHUNKS[ch]
            result = sb([P, PACK, width], F32, "result_%d" % ch)
            for t in range(PACK):
                nc.scalar.activation(out=result[:, t, :], in_=acc_slice(ch, t), func=GELU, bias=bias[:, t : t + 1])
            nc.sync.dma_start(out=out_rows[:, :, j0 : j0 + width], in_=result[:])
            results[ch] = result

        def hand_on(ch, engine):
            j0, width = CHUNKS[ch]
            words = sb([P, PACK * width], BF16, "out_words_%d" % ch)
            interleave(engine, words[:], results[ch][:])
            codes = sb([P, width], U32, "out_codes_%d" % ch)
            nc.vector.quantize_mx(out=codes[:].bitcast(FP8X4), scales=out_scales[:, j0 : j0 + width], in_=words[:])
            nc.sync.dma_start(
                out=out_words[:, PACK * j0 : PACK * (j0 + width)].bitcast(I32), in_=codes[:].bitcast(I32)
            )

        for quarter in range(2):
            first_tier(quarter, "scalar")
        for quarter in range(2):
            second_tier_on_vector(quarter)
        for quarter in range(2, 4):
            first_tier(quarter, "scalar")
        deal_words()
        for quarter in range(2, 4):
            second_tier_on_tensor(quarter)
        stage(0, 0, HALF, "c_0")
        stage(0, HALF, HALF, "c_1")
        for plane in range(2):
            gather(plane, 0, HALF)
            gather(plane, HALF, HALF)
        deal_scales()
        for plane in range(2, 4):
            gather(plane, 0, HALF)
            gather(plane, HALF, HALF)
            quantize_rest(plane, "x_%d" % plane)
        for ch in range(len(CHUNKS)):
            c_passes(ch)
        first_pass(0)
        first_pass(1)
        stage(1, 0, HALF)
        for plane in range(4, 7):
            gather(plane, 0, HALF)
        gather(7, 0, QUARTER)
        gather(7, QUARTER, QUARTER)
        second_pass(0, "scalar")
        second_pass(1, "scalar")
        stage_shared(512)
        stage_shared(768)
        for plane in range(4, 8):
            gather(plane, 512, 256)
        second_pass(2, "vector")
        activate(0)
        activate(1)
        for plane in range(4, 7):
            gather(plane, 768, 256)
        gather(7, 768, 128)
        gather(7, 896, 128)
        second_pass(3, "vector")
        second_pass(4, "vector")
        hand_on(0, "scalar")
        activate(2)
        hand_on(1, "scalar")
        activate(3)
        activate(4)
        hand_on(2, "vector")
        hand_on(3, "vector")
        hand_on(4, "vector")
        for q in range(4):
            queue = nc.sync if q % 2 == 0 else nc.scalar
            queue.dma_start(
                out=out_2[0, 4 * q : 4 * q + 4, :].bitcast(I32), in_=out_scales[32 * q : 32 * q + 4, :].bitcast(I32)
            )
